import numpy as np
import ml_dtypes


def mxq(x, axis, fmt="e4m3"):
    dtype, down = {"e4m3": (ml_dtypes.float8_e4m3fn, 7), "e5m2": (ml_dtypes.float8_e5m2, 14)}[fmt]
    v = np.moveaxis(np.asarray(x, np.float32).astype(ml_dtypes.bfloat16).astype(np.float64), axis, -1)
    blocks = v.reshape(v.shape[:-1] + (-1, 32))
    amax = np.abs(blocks).max(-1, keepdims=True)
    byte = np.maximum(np.where(amax > 0, np.frexp(amax)[1] - 1 + 127, 0) - down, 1)
    scale = np.exp2(byte - 127.0)
    codes = (blocks / scale).astype(np.float32).astype(dtype).astype(np.float64)
    return np.moveaxis((codes * scale).reshape(v.shape), -1, axis)


WIDE = False


def mx_kscale(k):
    if not WIDE:
        return np.ones(k)
    levels = np.array([10, -10, 5, -5, 0])
    if k % 512:
        return np.exp2(np.random.permutation(np.resize(levels, k // 32))).repeat(32)
    a = np.empty((k // 512, 16))
    for p in range(k // 512):
        a[p, :8] = np.random.permutation(np.resize(levels, 8))
        for g in range(8):
            far = levels[np.abs(levels - a[p, g]) >= 10]
            a[p, g + 8] = far[np.random.randint(len(far))]
    return np.exp2(a.ravel()).repeat(32)


BF16 = ml_dtypes.bfloat16


def bf(x):
    return np.asarray(x, np.float32).astype(BF16)


def f64(x):
    return np.asarray(x).astype(np.float64)


E2M1 = np.array([0.0, 0.5, 1.0, 1.5, 2.0, 3.0, 4.0, 6.0, -0.0, -0.5, -1.0, -1.5, -2.0, -3.0, -4.0, -6.0])


def pack_weight(w, fmt):
    k, n = w.shape
    w = f64(bf(w)).reshape(k // 32, 32, n)
    amax = np.abs(w).max(1)
    if fmt == "e4m3":
        byte = np.frexp(amax)[1] - 1 + 127 - 7
    else:
        mant, ex = np.frexp(amax / 6.0)
        byte = np.where(mant > 0.5, ex, ex - 1) + 127
    byte = np.clip(np.where(amax > 0, byte, 1), 1, 254)
    scaled = (w * np.exp2(127.0 - byte)[:, None, :]).reshape(k, n).astype(np.float32)
    by_word = np.ascontiguousarray(scaled.reshape(k // 512, 128, 4, n).transpose(0, 1, 3, 2))
    if fmt == "e4m3":
        words = by_word.astype(ml_dtypes.float8_e4m3fn).view(np.uint8)
    else:
        c = by_word.astype(ml_dtypes.float4_e2m1fn).view(np.uint8) & 0xF
        words = c[..., 0::2] | (c[..., 1::2] << 4)
    return np.ascontiguousarray(words), np.ascontiguousarray(byte.astype(np.uint8).reshape(k // 512, 16, n))


def unpack_weight(words, scales, fmt):
    g, p, n, _ = words.shape
    if fmt == "e4m3":
        vals = np.ascontiguousarray(words).view(ml_dtypes.float8_e4m3fn).astype(np.float64)
    else:
        nib = np.empty((g, p, n, 4), np.uint8)
        nib[..., 0::2] = words & 0xF
        nib[..., 1::2] = words >> 4
        vals = E2M1[nib]
    vals = vals * np.repeat(np.exp2(scales.astype(np.float64) - 127.0), 8, axis=1)[..., None]
    return vals.transpose(0, 1, 3, 2).reshape(g * 512, n)
def pack4(w):
    words, scales = pack_weight(w, "e2m1")
    return words.reshape(words.shape[0], 128, -1), scales


def unpack4(words, scales):
    return unpack_weight(words.reshape(words.shape[0], 128, -1, 2), scales, "e2m1")


M, D, C, H = 1024, 1536, 512, 1024


def draw0():
    s, u, t = mx_kscale(D), mx_kscale(C), mx_kscale(H)
    v_words, v_scales = pack4(np.random.standard_normal((C, H)) / np.sqrt(2 * C) / u[:, None])
    a_words, a_scales = pack4(np.random.standard_normal((H, D)) / np.sqrt(H) / t[:, None])
    return {"z": bf(np.random.standard_normal((M, D)) * s),
            "c": bf(np.random.standard_normal((M, C)) * u),
            "b": bf(np.random.standard_normal((D, H)) / np.sqrt(2 * D) / s[:, None]),
            "v_words": v_words, "v_scales": v_scales,
            "gain": bf((1 + 0.1 * np.random.standard_normal(H)) * t),
            "a_words": a_words, "a_scales": a_scales,
            "r": bf((1 + 0.1 * np.random.standard_normal(D)) / s)}


def core(z, c, b, v_words, v_scales, gain, a_words, a_scales, r):
    v = unpack4(v_words, v_scales)
    a = unpack4(a_words, a_scales)
    pre = ((mxq(f64(z), 1, "e4m3") @ mxq(f64(b), 0, "e4m3"))
           + (mxq(f64(c), 1, "e4m3") @ v))
    h = np.tanh(pre)
    y = h * f64(gain)
    z_new = f64(z) * f64(r) + (mxq(y, 1, "e4m3") @ a)
    slope = 1 - h * h
    return z_new, slope


def e4m3fn_bytes(y):
    return np.clip(np.asarray(y, np.float64), -448.0, 448.0).astype(np.float32).astype(ml_dtypes.float8_e4m3fn).view(np.uint8)


def e4m3fn_values(b):
    return np.asarray(b, np.uint8).view(ml_dtypes.float8_e4m3fn).astype(np.float64)


def setup_inputs():
    d = draw0()
    x0 = np.asarray(d['b']).astype(np.float64)
    s = (np.max(np.abs(x0), axis=(1,), keepdims=True) / 448.0).astype(np.float32)
    out = {}
    for k, v in d.items():
        if k == 'b':
            out['b_bytes'] = e4m3fn_bytes(x0 / s.astype(np.float64))
            out['b_scale'] = s
        else:
            out[k] = v
    return out


def reference(z, c, b_bytes, b_scale, v_words, v_scales, gain, a_words, a_scales, r):
    return core(z, c, e4m3fn_values(b_bytes) * b_scale.astype(np.float64), v_words, v_scales, gain, a_words, a_scales, r)

@@ -1,0 +1,299 @@
+from contextlib import ExitStack
+
+import concourse.mybir as mybir
+from concourse.masks import make_identity
+
+M, D, C, H = 1024, 1536, 512, 1024
+FLOPS = 2 * M * H * (D + C) + 2 * M * H * D
+
+F32 = mybir.dt.float32
+BF16 = mybir.dt.bfloat16
+I32 = mybir.dt.int32
+U32 = mybir.dt.uint32
+U8 = mybir.dt.uint8
+FP8 = mybir.dt.float8_e4m3fn
+FP8X4 = mybir.dt.float8_e4m3fn_x4
+FP4X4 = mybir.dt.float4_e2m1fn_x4
+ACT = mybir.ActivationFunctionType
+ALU = mybir.AluOpType
+
+P = 128
+BANK = 512
+NT = M // P
+GB = D // 512
+GY = H // 512
+ZD = D // BANK
+
+WIDEN_V = ((0, 0), (0, 1), (1, 0))
+ZR_V = 1024
+ONE_MINUS_G = ()
+
+
+def tile_sylvester_flow_step_s3_kernel(tc, z, c, b_bytes, b_scale, v_words, v_scales, gain, a_words, a_scales, r, out_0, out_1):
+    nc = tc.nc
+    with ExitStack() as ctx:
+        pool = ctx.enter_context(tc.tile_pool(name="sb", bufs=1))
+        psum = ctx.enter_context(tc.psum_pool(name="ps", bufs=1))
+        ctx.enter_context(tc.manual_schedule())
+
+        def sb(name, shape, dtype, bufs=1):
+            return pool.tile(shape, dtype, name=name, tag=name, bufs=bufs, align_bytes=64)
+
+        def bank(name, shape):
+            return psum.tile(shape, F32, name=name, tag=name, bufs=1)
+
+        warm = sb("warm", [P, 2], F32)
+        nc.vector.memset(warm[:], 0.0)
+        nc.scalar.activation(out=warm[:, 1:2], in_=warm[:, 0:1], func=ACT.Tanh)
+        v_sc = sb("v_sc", [P, H], U8)
+        a_sc = sb("a_sc", [P, GY * D], U8)
+        nc.vector.memset(v_sc[:].bitcast(I32), 0)
+        nc.vector.memset(a_sc[:].bitcast(I32), 0)
+        ident = sb("ident", [P, P], F32)
+        make_identity(nc, ident[:])
+
+        bs = sb("bs", [P, GB, 4], F32)
+        bb = [sb("bb%d" % g, [P, 4, H], U8) for g in range(GB)]
+        zt = [sb("z%d" % i, [P, D], BF16) for i in range(NT)]
+        ct = [sb("c%d" % i, [P, 4, C], BF16) for i in range(2)]
+        v_w = sb("v_w", [P, 2 * H], U8)
+        a_w = sb("a_w", [P, GY, 2 * D], U8)
+        gain_t = sb("gain_t", [P, H], BF16)
+        r_t = sb("r_t", [P, D], BF16)
+
+        b_rows = b_bytes.rearrange("(g p t) n -> g p t n", p=P, t=4)
+
+        def load_b(g):
+            nc.sync.dma_start(out=bb[g][:], in_=b_rows[g])
+
+        def load_z(i):
+            nc.sync.dma_start(out=zt[i][:], in_=z[i * P:(i + 1) * P, :])
+
+        def load_c(i):
+            nc.sync.dma_start(out=ct[i][:], in_=c[4 * i * P:4 * (i + 1) * P, :].rearrange("(i p) k -> p i k", p=P))
+
+        v_sc32 = v_sc[:].bitcast(I32)
+        v_src = v_scales.bitcast(I32)
+        a_sc32 = a_sc[:].bitcast(I32).rearrange("p (g n) -> p g n", g=GY)
+        a_src = a_scales.bitcast(I32).rearrange("g q n -> q g n")
+
+        nc.sync.dma_start(out=bs[:], in_=b_scale.rearrange("(g p t) o -> p g (t o)", p=P, t=4))
+        nc.sync.dma_start(out=bb[0][:, 0:2, :], in_=b_rows[0][:, 0:2, :])
+        nc.sync.dma_start(out=bb[0][:, 2:4, :], in_=b_rows[0][:, 2:4, :])
+        load_b(1)
+        load_b(2)
+        load_z(0)
+        load_c(0)
+        load_z(1)
+        nc.sync.dma_start(out=v_w[:], in_=v_words[0])
+        for q in range(4):
+            nc.sync.dma_start(out=v_sc32[32 * q:32 * q + 4, :], in_=v_src[0, 4 * q:4 * q + 4, :])
+        load_z(2)
+        load_z(3)
+        nc.sync.dma_start(out=gain_t[:], in_=gain.partition_broadcast(P))
+        nc.sync.dma_start(out=r_t[:], in_=r.partition_broadcast(P))
+        load_z(4)
+        load_c(1)
+        load_z(5)
+        nc.sync.dma_start(out=a_w[:], in_=a_words.rearrange("g p n -> p g n"))
+        for q in range(4):
+            nc.sync.dma_start(out=a_sc32[32 * q:32 * q + 4], in_=a_src[4 * q:4 * q + 4])
+        load_z(6)
+        load_z(7)
+
+        b_codes = [sb("b_codes%d" % g, [P, H], U32) for g in range(GB)]
+        b_sc = [sb("b_sc%d" % g, [P, H], U8) for g in range(GB)]
+        wide = [sb("wide%d" % g, [P, 4, H], BF16) for g in range(GB)]
+        bgrp = {}
+        zcodes, zsc, grp, pre, hid, ysb, ygrp, ycodes, ysc, res, zps, yps = ({} for unused in range(12))
+
+        def widen(g, t):
+            src = bb[g][:, t, :].bitcast(FP8)
+            if (g, t) in WIDEN_V:
+                nc.vector.tensor_scalar(out=wide[g][:, t, :], in0=src, scalar1=bs[:, g, t:t + 1], scalar2=None, op0=ALU.mult)
+            else:
+                nc.scalar.activation(out=wide[g][:, t, :], in_=src, func=ACT.Copy, scale=bs[:, g, t:t + 1])
+
+        def interleave(g, half):
+            if half == 0:
+                bgrp[g] = sb("bgrp", [P, 4 * H], BF16, bufs=2)
+            n0, n1 = half * 512, half * 512 + 512
+            nc.vector.tensor_copy(
+                out=bgrp[g][:, 4 * n0:4 * n1].rearrange("p (n t) -> p n t", t=4),
+                in_=wide[g][:, :, n0:n1].rearrange("p t n -> p n t"))
+
+        def quant_b(g):
+            nc.vector.quantize_mx(out=b_codes[g][:].bitcast(FP8X4), scales=b_sc[g][:], in_=bgrp[g][:])
+
+        def trans_z(i):
+            zw = zt[i][:].bitcast(F32)
+            cw = ct[i // 4][:, i % 4, :].bitcast(F32)
+            grp[i] = sb("grp", [P, 4 * BANK], BF16, bufs=3)
+            for half in range(2):
+                t_ps = bank("bank_t%d" % half, [P, 2, 2, P])
+                for gg in range(2):
+                    g = 2 * half + gg
+                    words = zw[:, 256 * g:256 * (g + 1)] if g < GB else cw
+                    for u in range(2):
+                        nc.tensor.transpose(t_ps[:, gg, u, :], words[:, u:256:2], ident[:])
+                nc.scalar.copy(
+                    out=grp[i][:].bitcast(F32)[:, BANK * half:BANK * (half + 1)].rearrange("p (g n u) -> p g n u", g=2, u=2),
+                    in_=t_ps[:].rearrange("p g u n -> p g n u"))
+
+        def quant_z(i):
+            zcodes[i] = sb("zcodes", [P, BANK], U32, bufs=NT)
+            zsc[i] = sb("zsc", [P, BANK], U8, bufs=NT)
+            nc.vector.quantize_mx(out=zcodes[i][:].bitcast(FP8X4), scales=zsc[i][:], in_=grp[i][:])
+
+        def open_pre(i):
+            names = ("bank_z0", "bank_z1") if i == 0 else ("bank_p0", "bank_p1")
+            pre[i] = [bank(nm, [P, BANK]) for nm in names]
+
+        def mm1(i, g, half):
+            k_cols = slice(P * g, P * (g + 1))
+            n_cols = slice(BANK * half, BANK * (half + 1))
+            if g == GB:
+                rhs, rhs_sc = v_w[:, 2 * BANK * half:2 * BANK * (half + 1)].bitcast(FP4X4), v_sc[:, n_cols]
+            else:
+                rhs, rhs_sc = b_codes[g][:, n_cols].bitcast(FP8X4), b_sc[g][:, n_cols]
+            nc.tensor.matmul_mx(out=pre[i][half][:], lhsT=zcodes[i][:, k_cols].bitcast(FP8X4), lhsT_scale=zsc[i][:, k_cols],
+                                rhs=rhs, rhs_scale=rhs_sc, start=(g == GB), stop=(g == GB - 1))
+
+        def mm1_all(i):
+            open_pre(i)
+            for half in range(2):
+                for g in (GB, 0, 1, 2):
+                    mm1(i, g, half)
+
+        def tanh(i):
+            hid[i] = sb("hid", [P, H], F32, bufs=3)
+            for half in range(2):
+                cols = slice(BANK * half, BANK * (half + 1))
+                nc.scalar.activation(out=hid[i][:, cols], in_=pre[i][half][:], func=ACT.Tanh)
+
+        def times_gain(i):
+            ysb[i] = sb("ysb", [P, H], BF16, bufs=3)
+            for g in range(GY):
+                cols = slice(BANK * g, BANK * (g + 1))
+                nc.vector.tensor_tensor(
+                    out=ysb[i][:, cols].rearrange("m (u p e) -> m u p e", u=2, e=2),
+                    in0=hid[i][:, cols].rearrange("m (p u e) -> m u p e", u=2, e=2),
+                    in1=gain_t[:, cols].rearrange("m (p u e) -> m u p e", u=2, e=2), op=ALU.mult)
+
+        def trans_y(i):
+            yw = ysb[i][:].bitcast(F32)
+            yps[i] = bank("bank_y", [P, GY, 2, P])
+            for g in range(GY):
+                for u in range(2):
+                    nc.tensor.transpose(yps[i][:, g, u, :], yw[:, 256 * g + P * u:256 * g + P * (u + 1)], ident[:])
+
+        def copy_y(i):
+            ygrp[i] = sb("ygrp", [P, 2 * BANK], BF16, bufs=2)
+            nc.scalar.copy(out=ygrp[i][:].bitcast(F32).rearrange("p (g n u) -> p g n u", g=GY, u=2),
+                           in_=yps[i][:].rearrange("p g u n -> p g n u"))
+
+        def quant_y(i):
+            ycodes[i] = sb("ycodes", [P, GY * P], U32, bufs=3)
+            ysc[i] = sb("ysc", [P, GY * P], U8, bufs=3)
+            nc.vector.quantize_mx(out=ycodes[i][:].bitcast(FP8X4), scales=ysc[i][:], in_=ygrp[i][:])
+
+        def mm2(i):
+            zps[i] = [bank("bank_z%d" % n, [P, BANK]) for n in range(ZD)]
+            for n in range(ZD):
+                for g in range(GY):
+                    nc.tensor.matmul_mx(
+                        out=zps[i][n][:], lhsT=ycodes[i][:, P * g:P * (g + 1)].bitcast(FP8X4), lhsT_scale=ysc[i][:, P * g:P * (g + 1)],
+                        rhs=a_w[:, g, 2 * BANK * n:2 * BANK * (n + 1)].bitcast(FP4X4),
+                        rhs_scale=a_sc[:, D * g + BANK * n:D * g + BANK * (n + 1)],
+                        start=(g == 0), stop=(g == GY - 1))
+
+        def times_r(i):
+            res[i] = sb("res", [P, D], F32, bufs=4)
+            nc.gpsimd.tensor_tensor(out=res[i][:, ZR_V:], in0=zt[i][:, ZR_V:], in1=r_t[:, ZR_V:], op=ALU.mult)
+            nc.vector.tensor_tensor(out=res[i][:, :ZR_V], in0=zt[i][:, :ZR_V], in1=r_t[:, :ZR_V], op=ALU.mult)
+
+        def add_z(i):
+            rows = slice(P * i, P * (i + 1))
+            for n in range(ZD):
+                cols = slice(BANK * n, BANK * (n + 1))
+                nc.vector.tensor_tensor(out=res[i][:, cols], in0=zps[i][n][:], in1=res[i][:, cols], op=ALU.add)
+                if i == NT - 1:
+                    nc.sync.dma_start(out=out_0[rows, cols], in_=res[i][:, cols])
+            if i < NT - 1:
+                nc.sync.dma_start(out=out_0[rows, :], in_=res[i][:])
+
+        def slope(i):
+            sq = sb("sq", [P, H], F32, bufs=3)
+            nc.scalar.activation(out=sq[:], in_=hid[i][:], func=ACT.Square)
+            if i in ONE_MINUS_G:
+                nc.gpsimd.tensor_scalar(out=sq[:], in0=sq[:], scalar1=-1.0, scalar2=1.0, op0=ALU.mult, op1=ALU.add)
+            else:
+                nc.scalar.activation(out=sq[:], in_=sq[:], func=ACT.Copy, scale=-1.0, bias=1.0)
+            nc.sync.dma_start(out=out_1[P * i:P * (i + 1), :], in_=sq[:])
+
+        for t in range(4):
+            widen(0, t)
+        for t in range(4):
+            widen(1, t)
+        trans_z(0)
+        interleave(0, 0)
+        interleave(0, 1)
+        for t in range(4):
+            widen(2, t)
+        quant_z(0)
+        quant_b(0)
+        interleave(1, 0)
+        interleave(1, 1)
+        trans_z(1)
+        open_pre(0)
+        for g in (GB, 0):
+            for half in range(2):
+                mm1(0, g, half)
+        trans_z(2)
+        quant_z(1)
+        quant_b(1)
+        interleave(2, 0)
+        interleave(2, 1)
+        open_pre(1)
+        for g in (GB, 0):
+            for half in range(2):
+                mm1(1, g, half)
+        trans_z(3)
+        quant_z(2)
+        quant_b(2)
+        for i in range(2):
+            for half in range(2):
+                mm1(i, 1, half)
+        trans_z(4)
+        quant_z(3)
+        times_r(0)
+        for half in range(2):
+            mm1(0, 2, half)
+        tanh(0)
+        times_gain(0)
+
+        for i in range(NT + 1):
+            if i + 1 < NT:
+                if i == 0:
+                    for half in range(2):
+                        mm1(1, 2, half)
+                else:
+                    mm1_all(i + 1)
+                tanh(i + 1)
+                times_gain(i + 1)
+            if i < NT:
+                trans_y(i)
+                copy_y(i)
+            if i + 5 < NT:
+                trans_z(i + 5)
+            if i < NT:
+                quant_y(i)
+            if i >= 1:
+                mm2(i - 1)
+                add_z(i - 1)
+            if i + 1 < NT:
+                times_r(i + 1)
+            if i + 4 < NT:
+                quant_z(i + 4)
+            if i < NT:
+                slope(i)

@@ -24,9 +24,189 @@ GB = D // 512
 GY = H // 512
 ZD = D // BANK
 
-WIDEN_V = ((0, 0), (0, 1), (1, 0))
-ZR_V = 1024
+WIDEN_V = ((0, 1), (0, 2), (0, 3), (1, 0), (2, 0))
+ZR_V = ((0, 1), (1, 0), (2, 1), (2, 2), (3, 2), (5, 2))
 ONE_MINUS_G = ()
+ONE_MINUS_V = (0, 1, 6)
+SPLIT_STORE = 0
+NTB = 3
+NZB = 2
+TEXT = (
+    ('w', 0, 0),
+    ('w', 0, 1),
+    ('spg',),
+    ('w', 1, 2),
+    ('w', 0, 2),
+    ('w', 1, 1),
+    ('w', 0, 3),
+    ('w', 1, 3),
+    ('il', 0, 0),
+    ('w', 2, 2),
+    ('il', 0, 1),
+    ('T', 0),
+    ('w', 2, 3),
+    ('w', 2, 1),
+    ('w', 1, 0),
+    ('qb', 0),
+    ('spr',),
+    ('w', 2, 0),
+    ('il', 1, 0),
+    ('Q', 0),
+    ('M1p', 0, (3, 0)),
+    ('T', 1),
+    ('il', 1, 1),
+    ('il', 2, 0),
+    ('il', 2, 1),
+    ('T', 2),
+    ('qb', 1),
+    ('qb', 2),
+    ('T', 3),
+    ('M1p', 0, (1, 2)),
+    ('Q', 1),
+    ('M1p', 1, (3, 0, 1, 2)),
+    ('tha', 0),
+    ('Y0', 0),
+    ('thb', 0),
+    ('Q', 2),
+    ('Y1', 0),
+    ('SQ', 0),
+    ('OM', 0),
+    ('ZR', 0),
+    ('tha', 1),
+    ('Y0', 1),
+    ('thb', 1),
+    ('YT', 0),
+    ('SQ', 1),
+    ('T', 4),
+    ('Y1', 1),
+    ('YQ', 0),
+    ('Q', 3),
+    ('OM', 1),
+    ('ZR', 1),
+    ('M1a', 2),
+    ('tha', 2),
+    ('M1b', 2),
+    ('Y0', 2),
+    ('M20', 0),
+    ('thb', 2),
+    ('YT', 1),
+    ('A0', 0),
+    ('SQ', 2),
+    ('T', 5),
+    ('M21', 0),
+    ('Y1', 2),
+    ('M22', 0),
+    ('A1', 0),
+    ('YQ', 1),
+    ('Q', 4),
+    ('A2', 0),
+    ('OM', 2),
+    ('ZR', 2),
+    ('M1a', 3),
+    ('tha', 3),
+    ('M1b', 3),
+    ('Y0', 3),
+    ('M20', 1),
+    ('thb', 3),
+    ('YT', 2),
+    ('A0', 1),
+    ('SQ', 3),
+    ('T', 6),
+    ('M21', 1),
+    ('Y1', 3),
+    ('M22', 1),
+    ('A1', 1),
+    ('YQ', 2),
+    ('Q', 5),
+    ('A2', 1),
+    ('OM', 3),
+    ('ZR', 3),
+    ('M1a', 4),
+    ('tha', 4),
+    ('M1b', 4),
+    ('Y0', 4),
+    ('M20', 2),
+    ('thb', 4),
+    ('YT', 3),
+    ('A0', 2),
+    ('SQ', 4),
+    ('T', 7),
+    ('M21', 2),
+    ('Y1', 4),
+    ('M22', 2),
+    ('A1', 2),
+    ('YQ', 3),
+    ('Q', 6),
+    ('A2', 2),
+    ('OM', 4),
+    ('ZR', 4),
+    ('M1a', 5),
+    ('tha', 5),
+    ('M1b', 5),
+    ('Y0', 5),
+    ('M20', 3),
+    ('thb', 5),
+    ('YT', 4),
+    ('A0', 3),
+    ('SQ', 5),
+    ('M21', 3),
+    ('Y1', 5),
+    ('M22', 3),
+    ('A1', 3),
+    ('YQ', 4),
+    ('Q', 7),
+    ('A2', 3),
+    ('OM', 5),
+    ('ZR', 5),
+    ('M1a', 6),
+    ('tha', 6),
+    ('M1b', 6),
+    ('Y0', 6),
+    ('M20', 4),
+    ('thb', 6),
+    ('YT', 5),
+    ('A0', 4),
+    ('SQ', 6),
+    ('M21', 4),
+    ('Y1', 6),
+    ('M22', 4),
+    ('A1', 4),
+    ('YQ', 5),
+    ('A2', 4),
+    ('OM', 6),
+    ('ZR', 6),
+    ('M1a', 7),
+    ('tha', 7),
+    ('M1b', 7),
+    ('Y0', 7),
+    ('M20', 5),
+    ('thb', 7),
+    ('YT', 6),
+    ('A0', 5),
+    ('SQ', 7),
+    ('M21', 5),
+    ('Y1', 7),
+    ('M22', 5),
+    ('A1', 5),
+    ('YQ', 6),
+    ('A2', 5),
+    ('OM', 7),
+    ('ZR', 7),
+    ('M20', 6),
+    ('YT', 7),
+    ('A0', 6),
+    ('M21', 6),
+    ('M22', 6),
+    ('A1', 6),
+    ('YQ', 7),
+    ('A2', 6),
+    ('M20', 7),
+    ('A0', 7),
+    ('M21', 7),
+    ('M22', 7),
+    ('A1', 7),
+    ('A2', 7),
+)
 
 
 def tile_sylvester_flow_step_s3_kernel(tc, z, c, b_bytes, b_scale, v_words, v_scales, gain, a_words, a_scales, r, out_0, out_1):
@@ -52,13 +232,17 @@ def tile_sylvester_flow_step_s3_kernel(tc, z, c, b_bytes, b_scale, v_words, v_sc
         ident = sb("ident", [P, P], F32)
         make_identity(nc, ident[:])
 
+        vec = sb("vec", [P, H + D], BF16)
+        nc.vector.memset(vec[:].bitcast(I32), 0)
+        ones = sb("ones", [P, P], BF16)
+        nc.vector.memset(ones[:], 1.0)
+
         bs = sb("bs", [P, GB, 4], F32)
         bb = [sb("bb%d" % g, [P, 4, H], U8) for g in range(GB)]
         zt = [sb("z%d" % i, [P, D], BF16) for i in range(NT)]
         ct = [sb("c%d" % i, [P, 4, C], BF16) for i in range(2)]
         v_w = sb("v_w", [P, 2 * H], U8)
         a_w = sb("a_w", [P, GY, 2 * D], U8)
-        gain_t = sb("gain_t", [P, H], BF16)
         r_t = sb("r_t", [P, D], BF16)
 
         b_rows = b_bytes.rearrange("(g p t) n -> g p t n", p=P, t=4)
@@ -80,6 +264,8 @@ def tile_sylvester_flow_step_s3_kernel(tc, z, c, b_bytes, b_scale, v_words, v_sc
         nc.sync.dma_start(out=bs[:], in_=b_scale.rearrange("(g p t) o -> p g (t o)", p=P, t=4))
         nc.sync.dma_start(out=bb[0][:, 0:2, :], in_=b_rows[0][:, 0:2, :])
         nc.sync.dma_start(out=bb[0][:, 2:4, :], in_=b_rows[0][:, 2:4, :])
+        nc.sync.dma_start(out=vec[0:1, :H], in_=gain.rearrange("(o n) -> o n", o=1))
+        nc.sync.dma_start(out=vec[0:1, H:], in_=r.rearrange("(o n) -> o n", o=1))
         load_b(1)
         load_b(2)
         load_z(0)
@@ -90,8 +276,6 @@ def tile_sylvester_flow_step_s3_kernel(tc, z, c, b_bytes, b_scale, v_words, v_sc
             nc.sync.dma_start(out=v_sc32[32 * q:32 * q + 4, :], in_=v_src[0, 4 * q:4 * q + 4, :])
         load_z(2)
         load_z(3)
-        nc.sync.dma_start(out=gain_t[:], in_=gain.partition_broadcast(P))
-        nc.sync.dma_start(out=r_t[:], in_=r.partition_broadcast(P))
         load_z(4)
         load_c(1)
         load_z(5)
@@ -105,7 +289,7 @@ def tile_sylvester_flow_step_s3_kernel(tc, z, c, b_bytes, b_scale, v_words, v_sc
         b_sc = [sb("b_sc%d" % g, [P, H], U8) for g in range(GB)]
         wide = [sb("wide%d" % g, [P, 4, H], BF16) for g in range(GB)]
         bgrp = {}
-        zcodes, zsc, grp, pre, hid, ysb, ygrp, ycodes, ysc, res, zps, yps = ({} for unused in range(12))
+        zcodes, zsc, grp, pre, hid, ysb, ygrp, ycodes, ysc, res, zps, yps, zg = ({} for unused in range(13))
 
         def widen(g, t):
             src = bb[g][:, t, :].bitcast(FP8)
@@ -113,6 +297,20 @@ def tile_sylvester_flow_step_s3_kernel(tc, z, c, b_bytes, b_scale, v_words, v_sc
                 nc.vector.tensor_scalar(out=wide[g][:, t, :], in0=src, scalar1=bs[:, g, t:t + 1], scalar2=None, op0=ALU.mult)
             else:
                 nc.scalar.activation(out=wide[g][:, t, :], in_=src, func=ACT.Copy, scale=bs[:, g, t:t + 1])
+
+        gain_ps = psum.tile([P, H], BF16, name="bank_g", tag="bank_g", bufs=1)
+
+        def spread_gain():
+            for c0 in range(0, H, BANK):
+                nc.tensor.matmul(out=gain_ps[:, c0:c0 + BANK], lhsT=ones[:], rhs=vec[:, c0:c0 + BANK], start=True, stop=True)
+
+        def spread_r():
+            for k in range(2):
+                lo, hi = H + 1024 * k, min(H + 1024 * k + 1024, H + D)
+                v_ps = psum.tile([P, 1024], BF16, name="bank_p%d" % k, tag="bank_p%d" % k, bufs=1)
+                for c0 in range(lo, hi, BANK):
+                    nc.tensor.matmul(out=v_ps[:, c0 - lo:c0 - lo + BANK], lhsT=ones[:], rhs=vec[:, c0:c0 + BANK], start=True, stop=True)
+                nc.scalar.copy(out=r_t[:, lo - H:hi - H], in_=v_ps[:, :hi - lo])
 
         def interleave(g, half):
             if half == 0:
@@ -125,12 +323,22 @@ def tile_sylvester_flow_step_s3_kernel(tc, z, c, b_bytes, b_scale, v_words, v_sc
         def quant_b(g):
             nc.vector.quantize_mx(out=b_codes[g][:].bitcast(FP8X4), scales=b_sc[g][:], in_=bgrp[g][:])
 
+        counts = {"t": 0, "z": 0}
+
+        def t_bank():
+            counts["t"] += 1
+            return "bank_t%d" % (counts["t"] % NTB)
+
+        def z_bank():
+            counts["z"] += 1
+            return "bank_z%d" % (counts["z"] % NZB)
+
         def trans_z(i):
             zw = zt[i][:].bitcast(F32)
             cw = ct[i // 4][:, i % 4, :].bitcast(F32)
             grp[i] = sb("grp", [P, 4 * BANK], BF16, bufs=3)
             for half in range(2):
-                t_ps = bank("bank_t%d" % half, [P, 2, 2, P])
+                t_ps = bank(t_bank(), [P, 2, 2, P])
                 for gg in range(2):
                     g = 2 * half + gg
                     words = zw[:, 256 * g:256 * (g + 1)] if g < GB else cw
@@ -159,30 +367,30 @@ def tile_sylvester_flow_step_s3_kernel(tc, z, c, b_bytes, b_scale, v_words, v_sc
             nc.tensor.matmul_mx(out=pre[i][half][:], lhsT=zcodes[i][:, k_cols].bitcast(FP8X4), lhsT_scale=zsc[i][:, k_cols],
                                 rhs=rhs, rhs_scale=rhs_sc, start=(g == GB), stop=(g == GB - 1))
 
-        def mm1_all(i):
-            open_pre(i)
-            for half in range(2):
-                for g in (GB, 0, 1, 2):
-                    mm1(i, g, half)
+        def mm1_half(i, half):
+            if half == 0:
+                open_pre(i)
+            for g in (GB, 0, 1, 2):
+                mm1(i, g, half)
 
-        def tanh(i):
-            hid[i] = sb("hid", [P, H], F32, bufs=3)
-            for half in range(2):
+        def tanh_half(i, half):
+                if half == 0:
+                    hid[i] = sb("hid", [P, H], F32, bufs=3)
                 cols = slice(BANK * half, BANK * (half + 1))
                 nc.scalar.activation(out=hid[i][:, cols], in_=pre[i][half][:], func=ACT.Tanh)
 
-        def times_gain(i):
-            ysb[i] = sb("ysb", [P, H], BF16, bufs=3)
-            for g in range(GY):
+        def gain_half(i, g):
+                if g == 0:
+                    ysb[i] = sb("ysb", [P, H], BF16, bufs=3)
                 cols = slice(BANK * g, BANK * (g + 1))
                 nc.vector.tensor_tensor(
                     out=ysb[i][:, cols].rearrange("m (u p e) -> m u p e", u=2, e=2),
                     in0=hid[i][:, cols].rearrange("m (p u e) -> m u p e", u=2, e=2),
-                    in1=gain_t[:, cols].rearrange("m (p u e) -> m u p e", u=2, e=2), op=ALU.mult)
+                    in1=gain_ps[:, cols].rearrange("m (p u e) -> m u p e", u=2, e=2), op=ALU.mult)
 
         def trans_y(i):
             yw = ysb[i][:].bitcast(F32)
-            yps[i] = bank("bank_y", [P, GY, 2, P])
+            yps[i] = bank(t_bank(), [P, GY, 2, P])
             for g in range(GY):
                 for u in range(2):
                     nc.tensor.transpose(yps[i][:, g, u, :], yw[:, 256 * g + P * u:256 * g + P * (u + 1)], ident[:])
@@ -197,103 +405,61 @@ def tile_sylvester_flow_step_s3_kernel(tc, z, c, b_bytes, b_scale, v_words, v_sc
             ysc[i] = sb("ysc", [P, GY * P], U8, bufs=3)
             nc.vector.quantize_mx(out=ycodes[i][:].bitcast(FP8X4), scales=ysc[i][:], in_=ygrp[i][:])
 
-        def mm2(i):
-            zps[i] = [bank("bank_z%d" % n, [P, BANK]) for n in range(ZD)]
-            for n in range(ZD):
-                for g in range(GY):
-                    nc.tensor.matmul_mx(
-                        out=zps[i][n][:], lhsT=ycodes[i][:, P * g:P * (g + 1)].bitcast(FP8X4), lhsT_scale=ysc[i][:, P * g:P * (g + 1)],
-                        rhs=a_w[:, g, 2 * BANK * n:2 * BANK * (n + 1)].bitcast(FP4X4),
-                        rhs_scale=a_sc[:, D * g + BANK * n:D * g + BANK * (n + 1)],
-                        start=(g == 0), stop=(g == GY - 1))
+        def mm2(i, n):
+            zps[i, n] = bank(z_bank(), [P, BANK])
+            for g in range(GY):
+                nc.tensor.matmul_mx(
+                    out=zps[i, n][:], lhsT=ycodes[i][:, P * g:P * (g + 1)].bitcast(FP8X4), lhsT_scale=ysc[i][:, P * g:P * (g + 1)],
+                    rhs=a_w[:, g, 2 * BANK * n:2 * BANK * (n + 1)].bitcast(FP4X4),
+                    rhs_scale=a_sc[:, D * g + BANK * n:D * g + BANK * (n + 1)],
+                    start=(g == 0), stop=(g == GY - 1))
 
         def times_r(i):
             res[i] = sb("res", [P, D], F32, bufs=4)
-            nc.gpsimd.tensor_tensor(out=res[i][:, ZR_V:], in0=zt[i][:, ZR_V:], in1=r_t[:, ZR_V:], op=ALU.mult)
-            nc.vector.tensor_tensor(out=res[i][:, :ZR_V], in0=zt[i][:, :ZR_V], in1=r_t[:, :ZR_V], op=ALU.mult)
-
-        def add_z(i):
-            rows = slice(P * i, P * (i + 1))
             for n in range(ZD):
                 cols = slice(BANK * n, BANK * (n + 1))
-                nc.vector.tensor_tensor(out=res[i][:, cols], in0=zps[i][n][:], in1=res[i][:, cols], op=ALU.add)
-                if i == NT - 1:
-                    nc.sync.dma_start(out=out_0[rows, cols], in_=res[i][:, cols])
-            if i < NT - 1:
-                nc.sync.dma_start(out=out_0[rows, :], in_=res[i][:])
+                eng = nc.vector if (i, n) in ZR_V else nc.gpsimd
+                eng.tensor_tensor(out=res[i][:, cols], in0=zt[i][:, cols], in1=r_t[:, cols], op=ALU.mult)
 
-        def slope(i):
-            sq = sb("sq", [P, H], F32, bufs=3)
-            nc.scalar.activation(out=sq[:], in_=hid[i][:], func=ACT.Square)
+        def add_bank(i, n):
+                rows = slice(P * i, P * (i + 1))
+                cols = slice(BANK * n, BANK * (n + 1))
+                in1 = res[i][:, cols]
+                nc.vector.tensor_tensor(out=res[i][:, cols], in0=zps[i, n][:], in1=in1, op=ALU.add)
+                if i >= SPLIT_STORE:
+                    nc.sync.dma_start(out=out_0[rows, cols], in_=res[i][:, cols])
+                elif n == ZD - 1:
+                    nc.sync.dma_start(out=out_0[rows, :], in_=res[i][:])
+
+        sqs = {}
+
+        def square(i):
+            sqs[i] = sb("sq", [P, H], F32, bufs=3)
+            nc.scalar.activation(out=sqs[i][:], in_=hid[i][:], func=ACT.Square)
+
+        def one_minus(i):
+            sq = sqs[i]
             if i in ONE_MINUS_G:
                 nc.gpsimd.tensor_scalar(out=sq[:], in0=sq[:], scalar1=-1.0, scalar2=1.0, op0=ALU.mult, op1=ALU.add)
+            elif i in ONE_MINUS_V:
+                nc.vector.tensor_scalar(out=sq[:], in0=sq[:], scalar1=-1.0, scalar2=1.0, op0=ALU.mult, op1=ALU.add)
             else:
                 nc.scalar.activation(out=sq[:], in_=sq[:], func=ACT.Copy, scale=-1.0, bias=1.0)
             nc.sync.dma_start(out=out_1[P * i:P * (i + 1), :], in_=sq[:])
 
-        for t in range(4):
-            widen(0, t)
-        for t in range(4):
-            widen(1, t)
-        trans_z(0)
-        interleave(0, 0)
-        interleave(0, 1)
-        for t in range(4):
-            widen(2, t)
-        quant_z(0)
-        quant_b(0)
-        interleave(1, 0)
-        interleave(1, 1)
-        trans_z(1)
-        open_pre(0)
-        for g in (GB, 0):
+        def zr(i):
+            times_r(i)
+        def mm1_part(i, gs):
+            if gs[0] == GB:
+                open_pre(i)
             for half in range(2):
-                mm1(0, g, half)
-        trans_z(2)
-        quant_z(1)
-        quant_b(1)
-        interleave(2, 0)
-        interleave(2, 1)
-        open_pre(1)
-        for g in (GB, 0):
-            for half in range(2):
-                mm1(1, g, half)
-        trans_z(3)
-        quant_z(2)
-        quant_b(2)
-        for i in range(2):
-            for half in range(2):
-                mm1(i, 1, half)
-        trans_z(4)
-        quant_z(3)
-        times_r(0)
-        for half in range(2):
-            mm1(0, 2, half)
-        tanh(0)
-        times_gain(0)
-
-        for i in range(NT + 1):
-            if i + 1 < NT:
-                if i == 0:
-                    for half in range(2):
-                        mm1(1, 2, half)
-                else:
-                    mm1_all(i + 1)
-                tanh(i + 1)
-                times_gain(i + 1)
-            if i < NT:
-                trans_y(i)
-                copy_y(i)
-            if i + 5 < NT:
-                trans_z(i + 5)
-            if i < NT:
-                quant_y(i)
-            if i >= 1:
-                mm2(i - 1)
-                add_z(i - 1)
-            if i + 1 < NT:
-                times_r(i + 1)
-            if i + 4 < NT:
-                quant_z(i + 4)
-            if i < NT:
-                slope(i)
+                for g in gs:
+                    mm1(i, g, half)
+        def il(g, half):
+            interleave(g, half)
+        table = {
+            "w": widen, "il": il, "qb": quant_b, "T": trans_z, "Q": quant_z, "M1p": mm1_part, "Y0": lambda i: gain_half(i, 0),
+            "Y1": lambda i: gain_half(i, 1), "YT": lambda i: (trans_y(i), copy_y(i)), "YQ": quant_y, "M20": lambda i: mm2(i, 0), "M21": lambda i: mm2(i, 1), "M22": lambda i: mm2(i, 2),
+            "A0": lambda i: add_bank(i, 0), "A1": lambda i: add_bank(i, 1), "A2": lambda i: add_bank(i, 2), "M1a": lambda i: mm1_half(i, 0), "M1b": lambda i: mm1_half(i, 1), "spg": spread_gain, "spr": spread_r, "ZR": times_r, "SQ": square, "OM": one_minus, "tha": lambda i: tanh_half(i, 0), "thb": lambda i: tanh_half(i, 1)}
+        for item in TEXT:
+            table[item[0]](*item[1:])

@@ -24,185 +24,210 @@ GB = D // 512
 GY = H // 512
 ZD = D // BANK
 
-WIDEN_V = ((0, 1), (0, 2), (0, 3), (1, 0), (2, 0))
-ZR_V = ((0, 1), (1, 0), (2, 1), (2, 2), (3, 2), (5, 2))
+LOADS = (('b0', 1), ('bs',), ('b0', 0), ('b', 1), ('vec',), ('b', 2), ('z', 1), ('z', 0), ('c', 0), ('v',), ('vs',), ('z', 2), ('z', 6), ('z', 3), ('c', 1), ('z', 4), ('z', 7), ('as',), ('z', 5), ('a',))
+WIDEN_V = ((0, 0, 1), (0, 1, 0), (0, 2, 0), (0, 2, 1), (1, 0, 0), (1, 2, 0), (1, 3, 0), (2, 0, 1), (2, 1, 0), (2, 1, 1))
+ZR_V = ((0, 0), (0, 1), (1, 0), (1, 2), (2, 0), (3, 1), (5, 0))
 ONE_MINUS_G = ()
-ONE_MINUS_V = (0, 1, 6)
+ONE_MINUS_V = (0, 1, 5)
 SPLIT_STORE = 0
 NTB = 3
-NZB = 2
+HB = 4
 TEXT = (
-    ('w', 0, 0),
-    ('w', 0, 1),
+    ('w', 0, 3, 0),
+    ('w', 0, 2, 0),
+    ('w', 0, 2, 1),
     ('spg',),
-    ('w', 1, 2),
-    ('w', 0, 2),
-    ('w', 1, 1),
-    ('w', 0, 3),
-    ('w', 1, 3),
+    ('w', 0, 0, 0),
+    ('w', 0, 1, 0),
+    ('w', 0, 0, 1),
     ('il', 0, 0),
-    ('w', 2, 2),
-    ('il', 0, 1),
-    ('T', 0),
-    ('w', 2, 3),
-    ('w', 2, 1),
-    ('w', 1, 0),
-    ('qb', 0),
-    ('spr',),
-    ('w', 2, 0),
+    ('w', 1, 3, 0),
+    ('w', 0, 3, 1),
+    ('w', 1, 1, 0),
+    ('w', 1, 2, 1),
+    ('w', 1, 2, 0),
+    ('w', 1, 0, 0),
+    ('qb', 0, 0),
+    ('w', 2, 1, 0),
     ('il', 1, 0),
-    ('Q', 0),
-    ('M1p', 0, (3, 0)),
-    ('T', 1),
-    ('il', 1, 1),
+    ('w', 2, 3, 0),
+    ('w', 2, 0, 1),
+    ('spr',),
+    ('qb', 1, 0),
+    ('w', 2, 2, 0),
+    ('w', 2, 0, 0),
     ('il', 2, 0),
-    ('il', 2, 1),
+    ('w', 0, 1, 1),
+    ('T', 0),
+    ('T', 1),
+    ('w', 2, 2, 1),
+    ('Q', 0),
+    ('qb', 2, 0),
+    ('w', 2, 1, 1),
     ('T', 2),
-    ('qb', 1),
-    ('qb', 2),
-    ('T', 3),
-    ('M1p', 0, (1, 2)),
+    ('w', 2, 3, 1),
     ('Q', 1),
-    ('M1p', 1, (3, 0, 1, 2)),
+    ('w', 1, 0, 1),
+    ('il', 0, 1),
+    ('w', 1, 1, 1),
+    ('Q', 2),
+    ('w', 1, 3, 1),
+    ('qb', 0, 1),
+    ('M1a', 0),
+    ('T', 3),
+    ('il', 2, 1),
+    ('il', 1, 1),
+    ('M1a', 1),
+    ('T', 4),
+    ('qb', 2, 1),
+    ('qb', 1, 1),
+    ('Q', 3),
+    ('T', 5),
+    ('Q', 4),
     ('tha', 0),
     ('Y0', 0),
-    ('thb', 0),
-    ('Q', 2),
-    ('Y1', 0),
-    ('SQ', 0),
-    ('OM', 0),
-    ('ZR', 0),
-    ('tha', 1),
-    ('Y0', 1),
-    ('thb', 1),
-    ('YT', 0),
-    ('SQ', 1),
-    ('T', 4),
-    ('Y1', 1),
-    ('YQ', 0),
-    ('Q', 3),
-    ('OM', 1),
-    ('ZR', 1),
-    ('M1a', 2),
-    ('tha', 2),
-    ('M1b', 2),
-    ('Y0', 2),
-    ('M20', 0),
-    ('thb', 2),
-    ('YT', 1),
-    ('A0', 0),
-    ('SQ', 2),
-    ('T', 5),
-    ('M21', 0),
-    ('Y1', 2),
-    ('M22', 0),
-    ('A1', 0),
-    ('YQ', 1),
-    ('Q', 4),
-    ('A2', 0),
-    ('OM', 2),
-    ('ZR', 2),
-    ('M1a', 3),
-    ('tha', 3),
-    ('M1b', 3),
-    ('Y0', 3),
-    ('M20', 1),
-    ('thb', 3),
-    ('YT', 2),
-    ('A0', 1),
-    ('SQ', 3),
-    ('T', 6),
-    ('M21', 1),
-    ('Y1', 3),
-    ('M22', 1),
-    ('A1', 1),
-    ('YQ', 2),
     ('Q', 5),
-    ('A2', 1),
-    ('OM', 3),
-    ('ZR', 3),
-    ('M1a', 4),
-    ('tha', 4),
-    ('M1b', 4),
-    ('Y0', 4),
-    ('M20', 2),
-    ('thb', 4),
-    ('YT', 3),
-    ('A0', 2),
-    ('SQ', 4),
-    ('T', 7),
-    ('M21', 2),
-    ('Y1', 4),
-    ('M22', 2),
-    ('A1', 2),
-    ('YQ', 3),
+    ('tha', 1),
+    ('T', 6),
+    ('Y0', 1),
+    ('M1b', 0),
     ('Q', 6),
-    ('A2', 2),
-    ('OM', 4),
-    ('ZR', 4),
-    ('M1a', 5),
-    ('tha', 5),
-    ('M1b', 5),
-    ('Y0', 5),
-    ('M20', 3),
-    ('thb', 5),
-    ('YT', 4),
-    ('A0', 3),
-    ('SQ', 5),
-    ('M21', 3),
-    ('Y1', 5),
-    ('M22', 3),
-    ('A1', 3),
-    ('YQ', 4),
+    ('M1a', 2),
+    ('thb', 0),
+    ('SQ0', 0),
+    ('tha', 2),
+    ('T', 7),
+    ('SQ1', 0),
+    ('Y1', 0),
+    ('Y0', 2),
+    ('M1b', 1),
     ('Q', 7),
-    ('A2', 3),
-    ('OM', 5),
-    ('ZR', 5),
+    ('OM', 0),
+    ('M1a', 3),
+    ('thb', 1),
+    ('SQ0', 1),
+    ('tha', 3),
+    ('SQ1', 1),
+    ('YT', 0),
+    ('Y1', 1),
+    ('Y0', 3),
+    ('M1b', 2),
+    ('OM', 1),
+    ('M1a', 4),
+    ('YQ', 0),
+    ('thb', 2),
+    ('SQ0', 2),
+    ('ZR', 0),
+    ('tha', 4),
+    ('SQ1', 2),
+    ('YT', 1),
+    ('Y1', 2),
+    ('Y0', 4),
+    ('M20', 0),
+    ('M1b', 3),
+    ('M21', 0),
+    ('A0', 0),
+    ('OM', 2),
+    ('M22', 0),
+    ('M1a', 5),
+    ('YQ', 1),
+    ('thb', 3),
+    ('SQ0', 3),
+    ('ZR', 1),
+    ('tha', 5),
+    ('A1', 0),
+    ('A2', 0),
+    ('SQ1', 3),
+    ('YT', 2),
+    ('Y1', 3),
+    ('Y0', 5),
+    ('M20', 1),
+    ('M1b', 4),
+    ('M21', 1),
+    ('A0', 1),
+    ('OM', 3),
+    ('M22', 1),
     ('M1a', 6),
+    ('YQ', 2),
+    ('thb', 4),
+    ('SQ0', 4),
+    ('ZR', 2),
     ('tha', 6),
-    ('M1b', 6),
+    ('A1', 1),
+    ('A2', 1),
+    ('SQ1', 4),
+    ('YT', 3),
+    ('Y1', 4),
     ('Y0', 6),
-    ('M20', 4),
-    ('thb', 6),
-    ('YT', 5),
-    ('A0', 4),
-    ('SQ', 6),
-    ('M21', 4),
-    ('Y1', 6),
-    ('M22', 4),
-    ('A1', 4),
-    ('YQ', 5),
-    ('A2', 4),
-    ('OM', 6),
-    ('ZR', 6),
+    ('M20', 2),
+    ('M1b', 5),
+    ('M21', 2),
+    ('A0', 2),
+    ('OM', 4),
+    ('M22', 2),
     ('M1a', 7),
+    ('YQ', 3),
+    ('thb', 5),
+    ('SQ0', 5),
+    ('ZR', 3),
     ('tha', 7),
-    ('M1b', 7),
+    ('A1', 2),
+    ('A2', 2),
+    ('SQ1', 5),
+    ('YT', 4),
+    ('Y1', 5),
     ('Y0', 7),
-    ('M20', 5),
+    ('M20', 3),
+    ('M1b', 6),
+    ('M21', 3),
+    ('A0', 3),
+    ('OM', 5),
+    ('M22', 3),
+    ('YQ', 4),
+    ('thb', 6),
+    ('SQ0', 6),
+    ('ZR', 4),
+    ('A1', 3),
+    ('A2', 3),
+    ('SQ1', 6),
+    ('YT', 5),
+    ('Y1', 6),
+    ('M20', 4),
+    ('M1b', 7),
+    ('M21', 4),
+    ('A0', 4),
+    ('OM', 6),
+    ('M22', 4),
+    ('YQ', 5),
     ('thb', 7),
+    ('SQ0', 7),
+    ('ZR', 5),
+    ('A1', 4),
+    ('A2', 4),
+    ('SQ1', 7),
     ('YT', 6),
-    ('A0', 5),
-    ('SQ', 7),
-    ('M21', 5),
     ('Y1', 7),
-    ('M22', 5),
-    ('A1', 5),
-    ('YQ', 6),
-    ('A2', 5),
+    ('M20', 5),
+    ('M21', 5),
+    ('A0', 5),
     ('OM', 7),
-    ('ZR', 7),
-    ('M20', 6),
+    ('M22', 5),
+    ('YQ', 6),
+    ('ZR', 6),
+    ('A1', 5),
+    ('A2', 5),
     ('YT', 7),
-    ('A0', 6),
+    ('M20', 6),
     ('M21', 6),
+    ('A0', 6),
     ('M22', 6),
-    ('A1', 6),
     ('YQ', 7),
+    ('ZR', 7),
+    ('A1', 6),
     ('A2', 6),
     ('M20', 7),
-    ('A0', 7),
     ('M21', 7),
+    ('A0', 7),
     ('M22', 7),
     ('A1', 7),
     ('A2', 7),
@@ -261,29 +286,33 @@ def tile_sylvester_flow_step_s3_kernel(tc, z, c, b_bytes, b_scale, v_words, v_sc
         a_sc32 = a_sc[:].bitcast(I32).rearrange("p (g n) -> p g n", g=GY)
         a_src = a_scales.bitcast(I32).rearrange("g q n -> q g n")
 
-        nc.sync.dma_start(out=bs[:], in_=b_scale.rearrange("(g p t) o -> p g (t o)", p=P, t=4))
-        nc.sync.dma_start(out=bb[0][:, 0:2, :], in_=b_rows[0][:, 0:2, :])
-        nc.sync.dma_start(out=bb[0][:, 2:4, :], in_=b_rows[0][:, 2:4, :])
-        nc.sync.dma_start(out=vec[0:1, :H], in_=gain.rearrange("(o n) -> o n", o=1))
-        nc.sync.dma_start(out=vec[0:1, H:], in_=r.rearrange("(o n) -> o n", o=1))
-        load_b(1)
-        load_b(2)
-        load_z(0)
-        load_c(0)
-        load_z(1)
-        nc.sync.dma_start(out=v_w[:], in_=v_words[0])
-        for q in range(4):
-            nc.sync.dma_start(out=v_sc32[32 * q:32 * q + 4, :], in_=v_src[0, 4 * q:4 * q + 4, :])
-        load_z(2)
-        load_z(3)
-        load_z(4)
-        load_c(1)
-        load_z(5)
-        nc.sync.dma_start(out=a_w[:], in_=a_words.rearrange("g p n -> p g n"))
-        for q in range(4):
-            nc.sync.dma_start(out=a_sc32[32 * q:32 * q + 4], in_=a_src[4 * q:4 * q + 4])
-        load_z(6)
-        load_z(7)
+        def load_v():
+            nc.sync.dma_start(out=v_w[:], in_=v_words[0])
+
+        def load_vs():
+            for q in range(4):
+                nc.sync.dma_start(out=v_sc32[32 * q:32 * q + 4, :], in_=v_src[0, 4 * q:4 * q + 4, :])
+
+        def load_a():
+            nc.sync.dma_start(out=a_w[:], in_=a_words.rearrange("g p n -> p g n"))
+
+        def load_as():
+            for q in range(4):
+                nc.sync.dma_start(out=a_sc32[32 * q:32 * q + 4], in_=a_src[4 * q:4 * q + 4])
+
+        def load_vec():
+            nc.sync.dma_start(out=vec[0:1, :H], in_=gain.rearrange("(o n) -> o n", o=1))
+            nc.sync.dma_start(out=vec[0:1, H:], in_=r.rearrange("(o n) -> o n", o=1))
+
+        def load_b0(k):
+            nc.sync.dma_start(out=bb[0][:, 2 * k:2 * k + 2, :], in_=b_rows[0][:, 2 * k:2 * k + 2, :])
+
+        def load_bs():
+            nc.sync.dma_start(out=bs[:], in_=b_scale.rearrange("(g p t) o -> p g (t o)", p=P, t=4))
+
+        ltab = {"bs": load_bs, "b0": load_b0, "b": load_b, "z": load_z, "c": load_c, "v": load_v, "vs": load_vs, "a": load_a, "as": load_as, "vec": load_vec}
+        for item in LOADS:
+            ltab[item[0]](*item[1:])
 
         b_codes = [sb("b_codes%d" % g, [P, H], U32) for g in range(GB)]
         b_sc = [sb("b_sc%d" % g, [P, H], U8) for g in range(GB)]
@@ -291,12 +320,13 @@ def tile_sylvester_flow_step_s3_kernel(tc, z, c, b_bytes, b_scale, v_words, v_sc
         bgrp = {}
         zcodes, zsc, grp, pre, hid, ysb, ygrp, ycodes, ysc, res, zps, yps, zg = ({} for unused in range(13))
 
-        def widen(g, t):
-            src = bb[g][:, t, :].bitcast(FP8)
-            if (g, t) in WIDEN_V:
-                nc.vector.tensor_scalar(out=wide[g][:, t, :], in0=src, scalar1=bs[:, g, t:t + 1], scalar2=None, op0=ALU.mult)
+        def widen(g, t, half):
+            cols = slice(BANK * half, BANK * (half + 1))
+            src = bb[g][:, t, cols].bitcast(FP8)
+            if (g, t, half) in WIDEN_V:
+                nc.vector.tensor_scalar(out=wide[g][:, t, cols], in0=src, scalar1=bs[:, g, t:t + 1], scalar2=None, op0=ALU.mult)
             else:
-                nc.scalar.activation(out=wide[g][:, t, :], in_=src, func=ACT.Copy, scale=bs[:, g, t:t + 1])
+                nc.scalar.activation(out=wide[g][:, t, cols], in_=src, func=ACT.Copy, scale=bs[:, g, t:t + 1])
 
         gain_ps = psum.tile([P, H], BF16, name="bank_g", tag="bank_g", bufs=1)
 
@@ -305,33 +335,33 @@ def tile_sylvester_flow_step_s3_kernel(tc, z, c, b_bytes, b_scale, v_words, v_sc
                 nc.tensor.matmul(out=gain_ps[:, c0:c0 + BANK], lhsT=ones[:], rhs=vec[:, c0:c0 + BANK], start=True, stop=True)
 
         def spread_r():
-            for k in range(2):
-                lo, hi = H + 1024 * k, min(H + 1024 * k + 1024, H + D)
-                v_ps = psum.tile([P, 1024], BF16, name="bank_p%d" % k, tag="bank_p%d" % k, bufs=1)
+            for lo, hi in ((0, 1024), (1024, D)):
+                nm = t_bank()
+                v_ps = psum.tile([P, 1024], BF16, name=nm, tag=nm, bufs=1)
                 for c0 in range(lo, hi, BANK):
-                    nc.tensor.matmul(out=v_ps[:, c0 - lo:c0 - lo + BANK], lhsT=ones[:], rhs=vec[:, c0:c0 + BANK], start=True, stop=True)
-                nc.scalar.copy(out=r_t[:, lo - H:hi - H], in_=v_ps[:, :hi - lo])
+                    nc.tensor.matmul(out=v_ps[:, c0 - lo:c0 - lo + BANK], lhsT=ones[:], rhs=vec[:, H + c0:H + c0 + BANK], start=True, stop=True)
+                nc.scalar.copy(out=r_t[:, lo:hi], in_=v_ps[:, :hi - lo])
 
-        def interleave(g, half):
-            if half == 0:
-                bgrp[g] = sb("bgrp", [P, 4 * H], BF16, bufs=2)
-            n0, n1 = half * 512, half * 512 + 512
-            nc.vector.tensor_copy(
-                out=bgrp[g][:, 4 * n0:4 * n1].rearrange("p (n t) -> p n t", t=4),
-                in_=wide[g][:, :, n0:n1].rearrange("p t n -> p n t"))
-
-        def quant_b(g):
-            nc.vector.quantize_mx(out=b_codes[g][:].bitcast(FP8X4), scales=b_sc[g][:], in_=bgrp[g][:])
-
-        counts = {"t": 0, "z": 0}
+        counts = {"t": 0, "m": 0}
 
         def t_bank():
             counts["t"] += 1
             return "bank_t%d" % (counts["t"] % NTB)
 
-        def z_bank():
-            counts["z"] += 1
-            return "bank_z%d" % (counts["z"] % NZB)
+        def m_bank():
+            counts["m"] += 1
+            return "bank_m%d" % (counts["m"] % (7 - NTB))
+
+        def interleave(g, half):
+            bgrp[g, half] = sb("bgrp", [P, 2 * H], BF16, bufs=3)
+            n0, n1 = half * 512, half * 512 + 512
+            nc.vector.tensor_copy(
+                out=bgrp[g, half][:].rearrange("p (n i t) -> p n t i", i=4, t=4),
+                in_=wide[g][:, :, n0:n1].rearrange("p t (n i) -> p n t i", i=4))
+
+        def quant_b(g, half):
+            cols = slice(BANK * half, BANK * (half + 1))
+            nc.vector.quantize_mx(out=b_codes[g][:, cols].bitcast(FP8X4), scales=b_sc[g][:, cols], in_=bgrp[g, half][:])
 
         def trans_z(i):
             zw = zt[i][:].bitcast(F32)
@@ -353,10 +383,6 @@ def tile_sylvester_flow_step_s3_kernel(tc, z, c, b_bytes, b_scale, v_words, v_sc
             zsc[i] = sb("zsc", [P, BANK], U8, bufs=NT)
             nc.vector.quantize_mx(out=zcodes[i][:].bitcast(FP8X4), scales=zsc[i][:], in_=grp[i][:])
 
-        def open_pre(i):
-            names = ("bank_z0", "bank_z1") if i == 0 else ("bank_p0", "bank_p1")
-            pre[i] = [bank(nm, [P, BANK]) for nm in names]
-
         def mm1(i, g, half):
             k_cols = slice(P * g, P * (g + 1))
             n_cols = slice(BANK * half, BANK * (half + 1))
@@ -364,20 +390,17 @@ def tile_sylvester_flow_step_s3_kernel(tc, z, c, b_bytes, b_scale, v_words, v_sc
                 rhs, rhs_sc = v_w[:, 2 * BANK * half:2 * BANK * (half + 1)].bitcast(FP4X4), v_sc[:, n_cols]
             else:
                 rhs, rhs_sc = b_codes[g][:, n_cols].bitcast(FP8X4), b_sc[g][:, n_cols]
-            nc.tensor.matmul_mx(out=pre[i][half][:], lhsT=zcodes[i][:, k_cols].bitcast(FP8X4), lhsT_scale=zsc[i][:, k_cols],
+            nc.tensor.matmul_mx(out=pre[i, half][:], lhsT=zcodes[i][:, k_cols].bitcast(FP8X4), lhsT_scale=zsc[i][:, k_cols],
                                 rhs=rhs, rhs_scale=rhs_sc, start=(g == GB), stop=(g == GB - 1))
 
         def mm1_half(i, half):
-            if half == 0:
-                open_pre(i)
+            pre[i, half] = bank(m_bank(), [P, BANK])
             for g in (GB, 0, 1, 2):
                 mm1(i, g, half)
 
         def tanh_half(i, half):
-                if half == 0:
-                    hid[i] = sb("hid", [P, H], F32, bufs=3)
-                cols = slice(BANK * half, BANK * (half + 1))
-                nc.scalar.activation(out=hid[i][:, cols], in_=pre[i][half][:], func=ACT.Tanh)
+            hid[i, half] = sb("hid%d" % half, [P, BANK], F32, bufs=HB)
+            nc.scalar.activation(out=hid[i, half][:], in_=pre[i, half][:], func=ACT.Tanh)
 
         def gain_half(i, g):
                 if g == 0:
@@ -385,7 +408,7 @@ def tile_sylvester_flow_step_s3_kernel(tc, z, c, b_bytes, b_scale, v_words, v_sc
                 cols = slice(BANK * g, BANK * (g + 1))
                 nc.vector.tensor_tensor(
                     out=ysb[i][:, cols].rearrange("m (u p e) -> m u p e", u=2, e=2),
-                    in0=hid[i][:, cols].rearrange("m (p u e) -> m u p e", u=2, e=2),
+                    in0=hid[i, g][:].rearrange("m (p u e) -> m u p e", u=2, e=2),
                     in1=gain_ps[:, cols].rearrange("m (p u e) -> m u p e", u=2, e=2), op=ALU.mult)
 
         def trans_y(i):
@@ -406,7 +429,7 @@ def tile_sylvester_flow_step_s3_kernel(tc, z, c, b_bytes, b_scale, v_words, v_sc
             nc.vector.quantize_mx(out=ycodes[i][:].bitcast(FP8X4), scales=ysc[i][:], in_=ygrp[i][:])
 
         def mm2(i, n):
-            zps[i, n] = bank(z_bank(), [P, BANK])
+            zps[i, n] = bank(m_bank(), [P, BANK])
             for g in range(GY):
                 nc.tensor.matmul_mx(
                     out=zps[i, n][:], lhsT=ycodes[i][:, P * g:P * (g + 1)].bitcast(FP8X4), lhsT_scale=ysc[i][:, P * g:P * (g + 1)],
@@ -433,9 +456,10 @@ def tile_sylvester_flow_step_s3_kernel(tc, z, c, b_bytes, b_scale, v_words, v_sc
 
         sqs = {}
 
-        def square(i):
-            sqs[i] = sb("sq", [P, H], F32, bufs=3)
-            nc.scalar.activation(out=sqs[i][:], in_=hid[i][:], func=ACT.Square)
+        def square(i, half):
+            if half == 0:
+                sqs[i] = sb("sq", [P, H], F32, bufs=3)
+            nc.scalar.activation(out=sqs[i][:, BANK * half:BANK * (half + 1)], in_=hid[i, half][:], func=ACT.Square)
 
         def one_minus(i):
             sq = sqs[i]
@@ -447,19 +471,10 @@ def tile_sylvester_flow_step_s3_kernel(tc, z, c, b_bytes, b_scale, v_words, v_sc
                 nc.scalar.activation(out=sq[:], in_=sq[:], func=ACT.Copy, scale=-1.0, bias=1.0)
             nc.sync.dma_start(out=out_1[P * i:P * (i + 1), :], in_=sq[:])
 
-        def zr(i):
-            times_r(i)
-        def mm1_part(i, gs):
-            if gs[0] == GB:
-                open_pre(i)
-            for half in range(2):
-                for g in gs:
-                    mm1(i, g, half)
-        def il(g, half):
-            interleave(g, half)
         table = {
-            "w": widen, "il": il, "qb": quant_b, "T": trans_z, "Q": quant_z, "M1p": mm1_part, "Y0": lambda i: gain_half(i, 0),
+            "w": widen, "il": interleave, "qb": quant_b, "T": trans_z, "Q": quant_z, "Y0": lambda i: gain_half(i, 0),
             "Y1": lambda i: gain_half(i, 1), "YT": lambda i: (trans_y(i), copy_y(i)), "YQ": quant_y, "M20": lambda i: mm2(i, 0), "M21": lambda i: mm2(i, 1), "M22": lambda i: mm2(i, 2),
-            "A0": lambda i: add_bank(i, 0), "A1": lambda i: add_bank(i, 1), "A2": lambda i: add_bank(i, 2), "M1a": lambda i: mm1_half(i, 0), "M1b": lambda i: mm1_half(i, 1), "spg": spread_gain, "spr": spread_r, "ZR": times_r, "SQ": square, "OM": one_minus, "tha": lambda i: tanh_half(i, 0), "thb": lambda i: tanh_half(i, 1)}
+            "A0": lambda i: add_bank(i, 0), "A1": lambda i: add_bank(i, 1), "A2": lambda i: add_bank(i, 2), "M1a": lambda i: mm1_half(i, 0), "M1b": lambda i: mm1_half(i, 1), "spg": spread_gain, "spr": spread_r, "ZR": times_r,
+            "SQ0": lambda i: square(i, 0), "SQ1": lambda i: square(i, 1), "OM": one_minus, "tha": lambda i: tanh_half(i, 0), "thb": lambda i: tanh_half(i, 1)}
         for item in TEXT:
             table[item[0]](*item[1:])

from contextlib import ExitStack

import concourse.mybir as mybir
from concourse.masks import make_identity

M, D, C, H = 1024, 1536, 512, 1024
FLOPS = 2 * M * H * (D + C) + 2 * M * H * D

F32 = mybir.dt.float32
BF16 = mybir.dt.bfloat16
I32 = mybir.dt.int32
U32 = mybir.dt.uint32
U8 = mybir.dt.uint8
FP8 = mybir.dt.float8_e4m3fn
FP8X4 = mybir.dt.float8_e4m3fn_x4
FP4X4 = mybir.dt.float4_e2m1fn_x4
ACT = mybir.ActivationFunctionType
ALU = mybir.AluOpType

P = 128
BANK = 512
NT = M // P
GB = D // 512
GY = H // 512
ZD = D // BANK

LOADS = (('b0', 1), ('bs',), ('b0', 0), ('b', 1), ('vec',), ('b', 2), ('z', 1), ('z', 0), ('c', 0), ('v',), ('vs',), ('z', 2), ('z', 6), ('z', 3), ('c', 1), ('z', 4), ('z', 7), ('as',), ('z', 5), ('a',))
WIDEN_V = ((0, 0, 1), (0, 1, 0), (0, 2, 0), (0, 2, 1), (1, 0, 0), (1, 2, 0), (1, 3, 0), (2, 0, 1), (2, 1, 0), (2, 1, 1))
ZR_V = ((0, 0), (0, 1), (1, 0), (1, 2), (2, 0), (3, 1), (5, 0))
ONE_MINUS_G = ()
ONE_MINUS_V = (0, 1, 5)
SPLIT_STORE = 0
NTB = 3
HB = 4
TEXT = (
    ('w', 0, 3, 0),
    ('w', 0, 2, 0),
    ('w', 0, 2, 1),
    ('spg',),
    ('w', 0, 0, 0),
    ('w', 0, 1, 0),
    ('w', 0, 0, 1),
    ('il', 0, 0),
    ('w', 1, 3, 0),
    ('w', 0, 3, 1),
    ('w', 1, 1, 0),
    ('w', 1, 2, 1),
    ('w', 1, 2, 0),
    ('w', 1, 0, 0),
    ('qb', 0, 0),
    ('w', 2, 1, 0),
    ('il', 1, 0),
    ('w', 2, 3, 0),
    ('w', 2, 0, 1),
    ('spr',),
    ('qb', 1, 0),
    ('w', 2, 2, 0),
    ('w', 2, 0, 0),
    ('il', 2, 0),
    ('w', 0, 1, 1),
    ('T', 0),
    ('T', 1),
    ('w', 2, 2, 1),
    ('Q', 0),
    ('qb', 2, 0),
    ('w', 2, 1, 1),
    ('T', 2),
    ('w', 2, 3, 1),
    ('Q', 1),
    ('w', 1, 0, 1),
    ('il', 0, 1),
    ('w', 1, 1, 1),
    ('Q', 2),
    ('w', 1, 3, 1),
    ('qb', 0, 1),
    ('M1a', 0),
    ('T', 3),
    ('il', 2, 1),
    ('il', 1, 1),
    ('M1a', 1),
    ('T', 4),
    ('qb', 2, 1),
    ('qb', 1, 1),
    ('Q', 3),
    ('T', 5),
    ('Q', 4),
    ('tha', 0),
    ('Y0', 0),
    ('Q', 5),
    ('tha', 1),
    ('T', 6),
    ('Y0', 1),
    ('M1b', 0),
    ('Q', 6),
    ('M1a', 2),
    ('thb', 0),
    ('SQ0', 0),
    ('tha', 2),
    ('T', 7),
    ('SQ1', 0),
    ('Y1', 0),
    ('Y0', 2),
    ('M1b', 1),
    ('Q', 7),
    ('OM', 0),
    ('M1a', 3),
    ('thb', 1),
    ('SQ0', 1),
    ('tha', 3),
    ('SQ1', 1),
    ('YT', 0),
    ('Y1', 1),
    ('Y0', 3),
    ('M1b', 2),
    ('OM', 1),
    ('M1a', 4),
    ('YQ', 0),
    ('thb', 2),
    ('SQ0', 2),
    ('ZR', 0),
    ('tha', 4),
    ('SQ1', 2),
    ('YT', 1),
    ('Y1', 2),
    ('Y0', 4),
    ('M20', 0),
    ('M1b', 3),
    ('M21', 0),
    ('A0', 0),
    ('OM', 2),
    ('M22', 0),
    ('M1a', 5),
    ('YQ', 1),
    ('thb', 3),
    ('SQ0', 3),
    ('ZR', 1),
    ('tha', 5),
    ('A1', 0),
    ('A2', 0),
    ('SQ1', 3),
    ('YT', 2),
    ('Y1', 3),
    ('Y0', 5),
    ('M20', 1),
    ('M1b', 4),
    ('M21', 1),
    ('A0', 1),
    ('OM', 3),
    ('M22', 1),
    ('M1a', 6),
    ('YQ', 2),
    ('thb', 4),
    ('SQ0', 4),
    ('ZR', 2),
    ('tha', 6),
    ('A1', 1),
    ('A2', 1),
    ('SQ1', 4),
    ('YT', 3),
    ('Y1', 4),
    ('Y0', 6),
    ('M20', 2),
    ('M1b', 5),
    ('M21', 2),
    ('A0', 2),
    ('OM', 4),
    ('M22', 2),
    ('M1a', 7),
    ('YQ', 3),
    ('thb', 5),
    ('SQ0', 5),
    ('ZR', 3),
    ('tha', 7),
    ('A1', 2),
    ('A2', 2),
    ('SQ1', 5),
    ('YT', 4),
    ('Y1', 5),
    ('Y0', 7),
    ('M20', 3),
    ('M1b', 6),
    ('M21', 3),
    ('A0', 3),
    ('OM', 5),
    ('M22', 3),
    ('YQ', 4),
    ('thb', 6),
    ('SQ0', 6),
    ('ZR', 4),
    ('A1', 3),
    ('A2', 3),
    ('SQ1', 6),
    ('YT', 5),
    ('Y1', 6),
    ('M20', 4),
    ('M1b', 7),
    ('M21', 4),
    ('A0', 4),
    ('OM', 6),
    ('M22', 4),
    ('YQ', 5),
    ('thb', 7),
    ('SQ0', 7),
    ('ZR', 5),
    ('A1', 4),
    ('A2', 4),
    ('SQ1', 7),
    ('YT', 6),
    ('Y1', 7),
    ('M20', 5),
    ('M21', 5),
    ('A0', 5),
    ('OM', 7),
    ('M22', 5),
    ('YQ', 6),
    ('ZR', 6),
    ('A1', 5),
    ('A2', 5),
    ('YT', 7),
    ('M20', 6),
    ('M21', 6),
    ('A0', 6),
    ('M22', 6),
    ('YQ', 7),
    ('ZR', 7),
    ('A1', 6),
    ('A2', 6),
    ('M20', 7),
    ('M21', 7),
    ('A0', 7),
    ('M22', 7),
    ('A1', 7),
    ('A2', 7),
)


def tile_sylvester_flow_step_s3_kernel(tc, z, c, b_bytes, b_scale, v_words, v_scales, gain, a_words, a_scales, r, out_0, out_1):
    nc = tc.nc
    with ExitStack() as ctx:
        pool = ctx.enter_context(tc.tile_pool(name="sb", bufs=1))
        psum = ctx.enter_context(tc.psum_pool(name="ps", bufs=1))
        ctx.enter_context(tc.manual_schedule())

        def sb(name, shape, dtype, bufs=1):
            return pool.tile(shape, dtype, name=name, tag=name, bufs=bufs, align_bytes=64)

        def bank(name, shape):
            return psum.tile(shape, F32, name=name, tag=name, bufs=1)

        warm = sb("warm", [P, 2], F32)
        nc.vector.memset(warm[:], 0.0)
        nc.scalar.activation(out=warm[:, 1:2], in_=warm[:, 0:1], func=ACT.Tanh)
        v_sc = sb("v_sc", [P, H], U8)
        a_sc = sb("a_sc", [P, GY * D], U8)
        nc.vector.memset(v_sc[:].bitcast(I32), 0)
        nc.vector.memset(a_sc[:].bitcast(I32), 0)
        ident = sb("ident", [P, P], F32)
        make_identity(nc, ident[:])

        vec = sb("vec", [P, H + D], BF16)
        nc.vector.memset(vec[:].bitcast(I32), 0)
        ones = sb("ones", [P, P], BF16)
        nc.vector.memset(ones[:], 1.0)

        bs = sb("bs", [P, GB, 4], F32)
        bb = [sb("bb%d" % g, [P, 4, H], U8) for g in range(GB)]
        zt = [sb("z%d" % i, [P, D], BF16) for i in range(NT)]
        ct = [sb("c%d" % i, [P, 4, C], BF16) for i in range(2)]
        v_w = sb("v_w", [P, 2 * H], U8)
        a_w = sb("a_w", [P, GY, 2 * D], U8)
        r_t = sb("r_t", [P, D], BF16)

        b_rows = b_bytes.rearrange("(g p t) n -> g p t n", p=P, t=4)

        def load_b(g):
            nc.sync.dma_start(out=bb[g][:], in_=b_rows[g])

        def load_z(i):
            nc.sync.dma_start(out=zt[i][:], in_=z[i * P:(i + 1) * P, :])

        def load_c(i):
            nc.sync.dma_start(out=ct[i][:], in_=c[4 * i * P:4 * (i + 1) * P, :].rearrange("(i p) k -> p i k", p=P))

        v_sc32 = v_sc[:].bitcast(I32)
        v_src = v_scales.bitcast(I32)
        a_sc32 = a_sc[:].bitcast(I32).rearrange("p (g n) -> p g n", g=GY)
        a_src = a_scales.bitcast(I32).rearrange("g q n -> q g n")

        def load_v():
            nc.sync.dma_start(out=v_w[:], in_=v_words[0])

        def load_vs():
            for q in range(4):
                nc.sync.dma_start(out=v_sc32[32 * q:32 * q + 4, :], in_=v_src[0, 4 * q:4 * q + 4, :])

        def load_a():
            nc.sync.dma_start(out=a_w[:], in_=a_words.rearrange("g p n -> p g n"))

        def load_as():
            for q in range(4):
                nc.sync.dma_start(out=a_sc32[32 * q:32 * q + 4], in_=a_src[4 * q:4 * q + 4])

        def load_vec():
            nc.sync.dma_start(out=vec[0:1, :H], in_=gain.rearrange("(o n) -> o n", o=1))
            nc.sync.dma_start(out=vec[0:1, H:], in_=r.rearrange("(o n) -> o n", o=1))

        def load_b0(k):
            nc.sync.dma_start(out=bb[0][:, 2 * k:2 * k + 2, :], in_=b_rows[0][:, 2 * k:2 * k + 2, :])

        def load_bs():
            nc.sync.dma_start(out=bs[:], in_=b_scale.rearrange("(g p t) o -> p g (t o)", p=P, t=4))

        ltab = {"bs": load_bs, "b0": load_b0, "b": load_b, "z": load_z, "c": load_c, "v": load_v, "vs": load_vs, "a": load_a, "as": load_as, "vec": load_vec}
        for item in LOADS:
            ltab[item[0]](*item[1:])

        b_codes = [sb("b_codes%d" % g, [P, H], U32) for g in range(GB)]
        b_sc = [sb("b_sc%d" % g, [P, H], U8) for g in range(GB)]
        wide = [sb("wide%d" % g, [P, 4, H], BF16) for g in range(GB)]
        bgrp = {}
        zcodes, zsc, grp, pre, hid, ysb, ygrp, ycodes, ysc, res, zps, yps, zg = ({} for unused in range(13))

        def widen(g, t, half):
            cols = slice(BANK * half, BANK * (half + 1))
            src = bb[g][:, t, cols].bitcast(FP8)
            if (g, t, half) in WIDEN_V:
                nc.vector.tensor_scalar(out=wide[g][:, t, cols], in0=src, scalar1=bs[:, g, t:t + 1], scalar2=None, op0=ALU.mult)
            else:
                nc.scalar.activation(out=wide[g][:, t, cols], in_=src, func=ACT.Copy, scale=bs[:, g, t:t + 1])

        gain_ps = psum.tile([P, H], BF16, name="bank_g", tag="bank_g", bufs=1)

        def spread_gain():
            for c0 in range(0, H, BANK):
                nc.tensor.matmul(out=gain_ps[:, c0:c0 + BANK], lhsT=ones[:], rhs=vec[:, c0:c0 + BANK], start=True, stop=True)

        def spread_r():
            for lo, hi in ((0, 1024), (1024, D)):
                nm = t_bank()
                v_ps = psum.tile([P, 1024], BF16, name=nm, tag=nm, bufs=1)
                for c0 in range(lo, hi, BANK):
                    nc.tensor.matmul(out=v_ps[:, c0 - lo:c0 - lo + BANK], lhsT=ones[:], rhs=vec[:, H + c0:H + c0 + BANK], start=True, stop=True)
                nc.scalar.copy(out=r_t[:, lo:hi], in_=v_ps[:, :hi - lo])

        counts = {"t": 0, "m": 0}

        def t_bank():
            counts["t"] += 1
            return "bank_t%d" % (counts["t"] % NTB)

        def m_bank():
            counts["m"] += 1
            return "bank_m%d" % (counts["m"] % (7 - NTB))

        def interleave(g, half):
            bgrp[g, half] = sb("bgrp", [P, 2 * H], BF16, bufs=3)
            n0, n1 = half * 512, half * 512 + 512
            nc.vector.tensor_copy(
                out=bgrp[g, half][:].rearrange("p (n i t) -> p n t i", i=4, t=4),
                in_=wide[g][:, :, n0:n1].rearrange("p t (n i) -> p n t i", i=4))

        def quant_b(g, half):
            cols = slice(BANK * half, BANK * (half + 1))
            nc.vector.quantize_mx(out=b_codes[g][:, cols].bitcast(FP8X4), scales=b_sc[g][:, cols], in_=bgrp[g, half][:])

        def trans_z(i):
            zw = zt[i][:].bitcast(F32)
            cw = ct[i // 4][:, i % 4, :].bitcast(F32)
            grp[i] = sb("grp", [P, 4 * BANK], BF16, bufs=3)
            for half in range(2):
                t_ps = bank(t_bank(), [P, 2, 2, P])
                for gg in range(2):
                    g = 2 * half + gg
                    words = zw[:, 256 * g:256 * (g + 1)] if g < GB else cw
                    for u in range(2):
                        nc.tensor.transpose(t_ps[:, gg, u, :], words[:, u:256:2], ident[:])
                nc.scalar.copy(
                    out=grp[i][:].bitcast(F32)[:, BANK * half:BANK * (half + 1)].rearrange("p (g n u) -> p g n u", g=2, u=2),
                    in_=t_ps[:].rearrange("p g u n -> p g n u"))

        def quant_z(i):
            zcodes[i] = sb("zcodes", [P, BANK], U32, bufs=NT)
            zsc[i] = sb("zsc", [P, BANK], U8, bufs=NT)
            nc.vector.quantize_mx(out=zcodes[i][:].bitcast(FP8X4), scales=zsc[i][:], in_=grp[i][:])

        def mm1(i, g, half):
            k_cols = slice(P * g, P * (g + 1))
            n_cols = slice(BANK * half, BANK * (half + 1))
            if g == GB:
                rhs, rhs_sc = v_w[:, 2 * BANK * half:2 * BANK * (half + 1)].bitcast(FP4X4), v_sc[:, n_cols]
            else:
                rhs, rhs_sc = b_codes[g][:, n_cols].bitcast(FP8X4), b_sc[g][:, n_cols]
            nc.tensor.matmul_mx(out=pre[i, half][:], lhsT=zcodes[i][:, k_cols].bitcast(FP8X4), lhsT_scale=zsc[i][:, k_cols],
                                rhs=rhs, rhs_scale=rhs_sc, start=(g == GB), stop=(g == GB - 1))

        def mm1_half(i, half):
            pre[i, half] = bank(m_bank(), [P, BANK])
            for g in (GB, 0, 1, 2):
                mm1(i, g, half)

        def tanh_half(i, half):
            hid[i, half] = sb("hid%d" % half, [P, BANK], F32, bufs=HB)
            nc.scalar.activation(out=hid[i, half][:], in_=pre[i, half][:], func=ACT.Tanh)

        def gain_half(i, g):
                if g == 0:
                    ysb[i] = sb("ysb", [P, H], BF16, bufs=3)
                cols = slice(BANK * g, BANK * (g + 1))
                nc.vector.tensor_tensor(
                    out=ysb[i][:, cols].rearrange("m (u p e) -> m u p e", u=2, e=2),
                    in0=hid[i, g][:].rearrange("m (p u e) -> m u p e", u=2, e=2),
                    in1=gain_ps[:, cols].rearrange("m (p u e) -> m u p e", u=2, e=2), op=ALU.mult)

        def trans_y(i):
            yw = ysb[i][:].bitcast(F32)
            yps[i] = bank(t_bank(), [P, GY, 2, P])
            for g in range(GY):
                for u in range(2):
                    nc.tensor.transpose(yps[i][:, g, u, :], yw[:, 256 * g + P * u:256 * g + P * (u + 1)], ident[:])

        def copy_y(i):
            ygrp[i] = sb("ygrp", [P, 2 * BANK], BF16, bufs=2)
            nc.scalar.copy(out=ygrp[i][:].bitcast(F32).rearrange("p (g n u) -> p g n u", g=GY, u=2),
                           in_=yps[i][:].rearrange("p g u n -> p g n u"))

        def quant_y(i):
            ycodes[i] = sb("ycodes", [P, GY * P], U32, bufs=3)
            ysc[i] = sb("ysc", [P, GY * P], U8, bufs=3)
            nc.vector.quantize_mx(out=ycodes[i][:].bitcast(FP8X4), scales=ysc[i][:], in_=ygrp[i][:])

        def mm2(i, n):
            zps[i, n] = bank(m_bank(), [P, BANK])
            for g in range(GY):
                nc.tensor.matmul_mx(
                    out=zps[i, n][:], lhsT=ycodes[i][:, P * g:P * (g + 1)].bitcast(FP8X4), lhsT_scale=ysc[i][:, P * g:P * (g + 1)],
                    rhs=a_w[:, g, 2 * BANK * n:2 * BANK * (n + 1)].bitcast(FP4X4),
                    rhs_scale=a_sc[:, D * g + BANK * n:D * g + BANK * (n + 1)],
                    start=(g == 0), stop=(g == GY - 1))

        def times_r(i):
            res[i] = sb("res", [P, D], F32, bufs=4)
            for n in range(ZD):
                cols = slice(BANK * n, BANK * (n + 1))
                eng = nc.vector if (i, n) in ZR_V else nc.gpsimd
                eng.tensor_tensor(out=res[i][:, cols], in0=zt[i][:, cols], in1=r_t[:, cols], op=ALU.mult)

        def add_bank(i, n):
                rows = slice(P * i, P * (i + 1))
                cols = slice(BANK * n, BANK * (n + 1))
                in1 = res[i][:, cols]
                nc.vector.tensor_tensor(out=res[i][:, cols], in0=zps[i, n][:], in1=in1, op=ALU.add)
                if i >= SPLIT_STORE:
                    nc.sync.dma_start(out=out_0[rows, cols], in_=res[i][:, cols])
                elif n == ZD - 1:
                    nc.sync.dma_start(out=out_0[rows, :], in_=res[i][:])

        sqs = {}

        def square(i, half):
            if half == 0:
                sqs[i] = sb("sq", [P, H], F32, bufs=3)
            nc.scalar.activation(out=sqs[i][:, BANK * half:BANK * (half + 1)], in_=hid[i, half][:], func=ACT.Square)

        def one_minus(i):
            sq = sqs[i]
            if i in ONE_MINUS_G:
                nc.gpsimd.tensor_scalar(out=sq[:], in0=sq[:], scalar1=-1.0, scalar2=1.0, op0=ALU.mult, op1=ALU.add)
            elif i in ONE_MINUS_V:
                nc.vector.tensor_scalar(out=sq[:], in0=sq[:], scalar1=-1.0, scalar2=1.0, op0=ALU.mult, op1=ALU.add)
            else:
                nc.scalar.activation(out=sq[:], in_=sq[:], func=ACT.Copy, scale=-1.0, bias=1.0)
            nc.sync.dma_start(out=out_1[P * i:P * (i + 1), :], in_=sq[:])

        table = {
            "w": widen, "il": interleave, "qb": quant_b, "T": trans_z, "Q": quant_z, "Y0": lambda i: gain_half(i, 0),
            "Y1": lambda i: gain_half(i, 1), "YT": lambda i: (trans_y(i), copy_y(i)), "YQ": quant_y, "M20": lambda i: mm2(i, 0), "M21": lambda i: mm2(i, 1), "M22": lambda i: mm2(i, 2),
            "A0": lambda i: add_bank(i, 0), "A1": lambda i: add_bank(i, 1), "A2": lambda i: add_bank(i, 2), "M1a": lambda i: mm1_half(i, 0), "M1b": lambda i: mm1_half(i, 1), "spg": spread_gain, "spr": spread_r, "ZR": times_r,
            "SQ0": lambda i: square(i, 0), "SQ1": lambda i: square(i, 1), "OM": one_minus, "tha": lambda i: tanh_half(i, 0), "thb": lambda i: tanh_half(i, 1)}
        for item in TEXT:
            table[item[0]](*item[1:])
